import numpy as np
CORES = [3,0,2,1,6,7,4,5]
N = 8
PERM = [[0,5],[1,3],[2,7],[3,0],[4,6],[5,2],[6,1],[7,4]]
def setup_inputs(rng):
    return {"x": rng.standard_normal((N, 128, 2), dtype=np.float32)}
def reference(x):
    y = np.empty_like(x)
    for s, d in PERM:
        y[d] = x[s]
    return {"y": y}

SCRATCH = {
    "send": ("sbuf", [128, 2], "float32"),
    "land": ("sbuf", [128, 2], "float32"),
}
SEMAPHORES = ["loaded", "read", "arrived", "stored"]


def engines(mask):
    return bin(mask).count("1")


def rank_program(g, core, T, topo):
    rank = T.rank_of(core)
    if rank is None:
        return
    perm = T.tables["PERM"]
    dst_rank = [d for s, d in perm if s == rank]
    src_rank = [s for s, d in perm if d == rank]

    if dst_rank:
        g.dma_start(T.send[:], T.x[:]).then_inc(T.sem.loaded, 16)
        g.wait_ge(T.sem.loaded, 16)

    sent = 0
    if dst_rank and dst_rank[0] != rank:
        dst = T.cores[dst_rank[0]]
        rid, pid = topo.addr(dst)[:2]
        m = topo.mask(core, dst)
        g.remote_dma(T.land[:], T.send[:], T.sem.arrived, T.sem.read, pid, rid, m)
        sent = engines(m)

    if src_rank:
        if src_rank[0] == rank:
            g.dma_start(T.y[:], T.send[:]).then_inc(T.sem.stored, 16)
        else:
            src = T.cores[src_rank[0]]
            g.wait_ge(T.sem.arrived, engines(topo.mask(src, core)))
            g.dma_start(T.y[:], T.land[:]).then_inc(T.sem.stored, 16)
        g.wait_ge(T.sem.stored, 16)

    if sent:
        g.wait_ge(T.sem.read, sent)
